import numpy as np
import ml_dtypes


def mxq(x, axis, fmt="e4m3"):
    dtype, down = {"e4m3": (ml_dtypes.float8_e4m3fn, 7), "e5m2": (ml_dtypes.float8_e5m2, 14)}[fmt]
    v = np.moveaxis(np.asarray(x, np.float32).astype(ml_dtypes.bfloat16).astype(np.float64), axis, -1)
    blocks = v.reshape(v.shape[:-1] + (-1, 32))
    amax = np.abs(blocks).max(-1, keepdims=True)
    byte = np.maximum(np.where(amax > 0, np.frexp(amax)[1] - 1 + 127, 0) - down, 1)
    scale = np.exp2(byte - 127.0)
    codes = (blocks / scale).astype(np.float32).astype(dtype).astype(np.float64)
    return np.moveaxis((codes * scale).reshape(v.shape), -1, axis)


WIDE = False


def mx_kscale(k):
    if not WIDE:
        return np.ones(k)
    levels = np.array([10, -10, 5, -5, 0])
    if k % 512:
        return np.exp2(np.random.permutation(np.resize(levels, k // 32))).repeat(32)
    a = np.empty((k // 512, 16))
    for p in range(k // 512):
        a[p, :8] = np.random.permutation(np.resize(levels, 8))
        for g in range(8):
            far = levels[np.abs(levels - a[p, g]) >= 10]
            a[p, g + 8] = far[np.random.randint(len(far))]
    return np.exp2(a.ravel()).repeat(32)


def f64(x):
    return np.asarray(x).astype(np.float64)


def striped(idx):
    return np.tile(idx.reshape(-1, 16).T, (8, 1)).astype(np.uint16)


def unstriped(offs):
    return offs[:16].T.reshape(-1).astype(np.int64)


E2M1 = np.array([0.0, 0.5, 1.0, 1.5, 2.0, 3.0, 4.0, 6.0, -0.0, -0.5, -1.0, -1.5, -2.0, -3.0, -4.0, -6.0])


def pack_weight(w, fmt):
    k, n = w.shape
    w = f64(np.asarray(w, np.float32).astype(ml_dtypes.bfloat16)).reshape(k // 32, 32, n)
    amax = np.abs(w).max(1)
    if fmt == "e4m3":
        byte = np.frexp(amax)[1] - 1 + 127 - 7
    else:
        mant, ex = np.frexp(amax / 6.0)
        byte = np.where(mant > 0.5, ex, ex - 1) + 127
    byte = np.clip(np.where(amax > 0, byte, 1), 1, 254)
    scaled = (w * np.exp2(127.0 - byte)[:, None, :]).reshape(k, n).astype(np.float32)
    by_word = np.ascontiguousarray(scaled.reshape(k // 512, 128, 4, n).transpose(0, 1, 3, 2))
    if fmt == "e4m3":
        words = by_word.astype(ml_dtypes.float8_e4m3fn).view(np.uint8)
    else:
        c = by_word.astype(ml_dtypes.float4_e2m1fn).view(np.uint8) & 0xF
        words = (c[..., 0::2] | (c[..., 1::2] << 4)).reshape(k // 512, 128, 2 * n)
    return np.ascontiguousarray(words), np.ascontiguousarray(byte.astype(np.uint8).reshape(k // 512, 16, n))


def unpack_weight(words, scales, fmt):
    g, _, n = scales.shape
    words = np.ascontiguousarray(words).reshape(g, 128, n, -1)
    if fmt == "e4m3":
        vals = words.view(ml_dtypes.float8_e4m3fn).astype(np.float64)
    else:
        nib = np.empty((g, 128, n, 4), np.uint8)
        nib[..., 0::2] = words & 0xF
        nib[..., 1::2] = words >> 4
        vals = E2M1[nib]
    vals = vals * np.repeat(np.exp2(scales.astype(np.float64) - 127.0), 8, axis=1)[..., None]
    return vals.transpose(0, 1, 3, 2).reshape(g * 512, n)


def gelu(v):
    return 0.5 * v * (1.0 + np.tanh(np.sqrt(2.0 / np.pi) * (v + 0.044715 * v**3)))


K, H, N, T, S, T2, P = 1536, 512, 512, 4096, 1024, 2048, 512

def setup_inputs():
    n = np.random.standard_normal
    s = mx_kscale(K)[:, None]
    u = mx_kscale(H)[:, None]
    tab_words, tab_scales = pack_weight(n((K, T)) * s, "e4m3")
    w4_words, w4_scales = pack_weight(n((H, N)) / np.sqrt(H) / u, "e2m1")
    perm = np.random.permutation(T2)
    return {
        "tab_words": tab_words, "tab_scales": tab_scales,
        "offs": striped(np.random.permutation(T)[:S]),
        "offs2": striped(np.random.permutation(T2)[:S]),
        "offs3": striped(perm[:P]),
        "offs4": striped(perm[P:2 * P]),
        "w1": (n((K, H)) / np.sqrt(K) / s).astype(np.float32),
        "cap": (0.3 + 0.6 * n(H)).astype(np.float32),
        "gain": (np.exp(0.3 * n(H)) * u[:, 0]).astype(np.float32),
        "wgs": np.exp(0.3 * n((128, S))).astype(np.float32),
        "page0": (n((H, T2)) * u).astype(np.float32),
        "lean": np.random.uniform(0.3, 1.8, H).astype(np.float32),
        "w4_words": w4_words, "w4_scales": w4_scales,
        "w5": (n((H, N)) / np.sqrt(H) / u).astype(np.float32),
        "bias": (0.5 * n(N)).astype(np.float32),
    }

def reference(tab_words, tab_scales, offs, offs2, offs3, offs4, w1, cap, gain, wgs, page0, lean, w4_words, w4_scales, w5, bias):
    v = unpack_weight(tab_words, tab_scales, "e4m3")[:, unstriped(offs)]
    x = mxq(f64(w1), 0, "e4m3").T @ v
    h = f64(gain)[:, None] * np.minimum(x, f64(cap)[:, None])
    page = f64(page0).copy()
    page[:, unstriped(offs2)] = np.tile(f64(wgs), (H // 128, 1)) * h
    port = page[:, unstriped(offs3)]
    star = page[:, unstriped(offs4)]
    both = port + star
    page[:, unstriped(offs3)] = both
    page[:, unstriped(offs4)] = np.maximum(both, f64(lean)[:, None] * port)
    d = mxq(page, 0, "e4m3")
    y4 = unpack_weight(w4_words, w4_scales, "e2m1").T @ d
    y5 = mxq(f64(w5), 0, "e4m3").T @ d
    return np.maximum(y4, y5) + f64(bias)[:, None]

@@ -1,0 +1,245 @@
+from contextlib import ExitStack
+
+import concourse.mybir as mybir
+
+K, H, N, T, S, T2, PAIRS = 1536, 512, 512, 4096, 1024, 2048, 512
+FLOPS = 2 * K * H * S + 2 * 2 * H * N * T2
+
+F32 = mybir.dt.float32
+BF16 = mybir.dt.bfloat16
+I32 = mybir.dt.int32
+U32 = mybir.dt.uint32
+U16 = mybir.dt.uint16
+U8 = mybir.dt.uint8
+FP8X4 = mybir.dt.float8_e4m3fn_x4
+FP4X4 = mybir.dt.float4_e2m1fn_x4
+ALU = mybir.AluOpType
+COPY = mybir.ActivationFunctionType.Copy
+IDENTITY = mybir.ActivationFunctionType.Identity
+
+P = 128
+PACK = 4
+K_PASS = P * PACK
+PASSES = K // K_PASS
+BANK = 512
+HALVES = S // BANK
+CHUNKS = T2 // BANK
+QUAD = 32
+LIST_COLS = BANK // 16
+
+
+def tile_list_ferry_bay_marshalling_kernel(
+    tc, tab_words, tab_scales, offs, offs2, offs3, offs4, w1, cap, gain, wgs, page0, lean, w4_words, w4_scales, w5, bias, out
+):
+    nc = tc.nc
+    with ExitStack() as ctx:
+        keep = ctx.enter_context(tc.tile_pool(name="keep", bufs=1))
+        ring = ctx.enter_context(tc.tile_pool(name="ring", bufs=2))
+        psum = ctx.enter_context(tc.psum_pool(name="psum", bufs=8))
+
+        def held(shape, dtype, name):
+            return keep.tile(shape, dtype, name=name, align_bytes=64)
+
+        def load_list(src, name):
+            t = keep.tile(list(src.shape), U16, name=name)
+            nc.sync.dma_start(t[:], src)
+            return t
+
+        def load_rows(vec, name):
+            t = held([P, PACK], F32, name)
+            nc.sync.dma_start(out=t[:], in_=vec.rearrange("(p t) -> p t", t=PACK))
+            return t
+
+        def load_weight(rows):
+            raw = ring.tile([P, PACK, H], F32, name="raw", tag="raw", bufs=3, align_bytes=64)
+            nc.sync.dma_start(out=raw[:], in_=rows.rearrange("(p j) c -> p j c", j=PACK))
+            return raw
+
+        def load_table(a):
+            t = held([P, T], I32, f"table{a}")
+            nc.sync.dma_start(out=t[:], in_=tab_words[a].rearrange("p t i -> p (t i)").bitcast(I32))
+            return t
+
+        def load_page(t):
+            pg = held([P, T2], F32, f"page{t}")
+            nc.sync.dma_start(out=pg[:], in_=page0.rearrange("(p t) c -> t p c", t=PACK)[t])
+            return pg
+
+        def load_wgs(t0, t1, name):
+            w = held([P, t1 - t0, S], F32, name)
+            src = wgs.rearrange("(q t) j -> q t j", t=PACK)[:, t0:t1, :]
+            for q in range(P // QUAD):
+                nc.sync.dma_start(out=w[QUAD * q : QUAD * (q + 1), :, :], in_=src)
+            return w
+
+        def quantise(grouped, name):
+            codes = held([P, BANK], U32, name + "_codes")
+            scales = held([P, BANK], U8, name + "_scales")
+            nc.vector.quantize_mx(out=codes[:].bitcast(FP8X4), scales=scales[:], in_=grouped)
+            return codes, scales
+
+        table_scales = held([P, T], U8, "table_scales")
+        nc.vector.memset(table_scales[:].bitcast(I32), 0)
+        w4_plane = held([P, N], U8, "w4_plane")
+        nc.vector.memset(w4_plane[:].bitcast(I32), 0)
+
+        picks = load_list(offs, "picks")
+        table = [load_table(0)]
+        for q in range(P // QUAD):
+            nc.sync.dma_start(
+                out=table_scales[QUAD * q : QUAD * q + 4 * PASSES, :].bitcast(I32),
+                in_=tab_scales[:, 4 * q : 4 * q + 4, :].bitcast(I32),
+            )
+        w1_raw = [load_weight(w1[0:K_PASS, :])]
+        table.append(load_table(1))
+        w1_raw.append(load_weight(w1[K_PASS : 2 * K_PASS, :]))
+        w1_raw.append(load_weight(w1[2 * K_PASS : 3 * K_PASS, :]))
+        cap_sb = load_rows(cap, "cap")
+        gain_sb = load_rows(gain, "gain")
+        table.append(load_table(2))
+        bays = load_list(offs2, "bays")
+        wgs_first = load_wgs(0, 1, "wgs_first")
+        pages = [load_page(0)]
+        ports = load_list(offs3, "ports")
+        stars = load_list(offs4, "stars")
+        lean_sb = load_rows(lean, "lean")
+        pages.append(load_page(1))
+        wgs_rest = load_wgs(1, PACK, "wgs_rest")
+        pages.append(load_page(2))
+        pages.append(load_page(3))
+        wgs_of = [wgs_first[:, 0, :]] + [wgs_rest[:, t, :] for t in range(PACK - 1)]
+
+        picked = [held([P, S], U32, f"picked{a}") for a in range(PASSES)]
+        picked_scales = held([P, S], U8, "picked_scales")
+        x_banks = [[psum.tile([P, BANK], F32, name="bank", tag="bank") for half in range(HALVES)] for t in range(PACK)]
+        for a in range(PASSES):
+            window = table[a][:].bitcast(U32)
+            if a < PASSES - 1:
+                nc.vector.tensor_copy(picked[a][:], window.indirect(picks[:]))
+            if a == 0:
+                nc.vector.tensor_copy(picked_scales[:], table_scales[:].indirect(picks[:]))
+            grouped = ring.tile([P, PACK * H], BF16, name="grouped", tag="grouped", align_bytes=64)
+            nc.scalar.copy(
+                out=grouped[:].rearrange("p (t m j) -> p m j t", t=PACK, j=PACK),
+                in_=w1_raw[a][:].rearrange("p j (m t) -> p m j t", t=PACK),
+            )
+            w1_codes, w1_scales = quantise(grouped[:], f"w1_{a}")
+            for half in range(HALVES):
+                cols = slice(BANK * half, BANK * (half + 1))
+                if a == PASSES - 1:
+                    nc.vector.tensor_copy(
+                        picked[a][:, cols], window.indirect(picks[:, LIST_COLS * half : LIST_COLS * (half + 1)])
+                    )
+                for t in range(PACK):
+                    rows = slice(P * t, P * (t + 1))
+                    nc.tensor.matmul_mx(
+                        out=x_banks[t][half][:],
+                        lhsT=w1_codes[:, rows].bitcast(FP8X4),
+                        lhsT_scale=w1_scales[:, rows],
+                        rhs=picked[a][:, cols].bitcast(FP8X4),
+                        rhs_scale=picked_scales[4 * a : P, cols],
+                        start=(a == 0),
+                        stop=(a == PASSES - 1),
+                    )
+
+        w5_raw = load_weight(w5)
+        w4_sb = held([P, 2 * N], U8, "w4")
+        nc.sync.dma_start(out=w4_sb[:].bitcast(I32), in_=w4_words[0].bitcast(I32))
+        for q in range(P // QUAD):
+            nc.sync.dma_start(
+                out=w4_plane[QUAD * q : QUAD * q + 4, :].bitcast(I32),
+                in_=w4_scales[0, 4 * q : 4 * q + 4, :].bitcast(I32),
+            )
+        bias_sb = held([P, N // P], F32, "bias")
+        with nc.allow_non_contiguous_dma(reason="one bias value to a partition"):
+            nc.sync.dma_start(out=bias_sb[:], in_=bias.rearrange("(j p) -> p j", p=P))
+
+        def h_tile():
+            return ring.tile([P, S], F32, name="h", tag="h")
+
+        def limit(t, dst, src):
+            nc.vector.tensor_scalar(dst, src, cap_sb[:, t : t + 1], gain_sb[:, t : t + 1], ALU.min, ALU.mult)
+
+        def evacuate(t):
+            h = h_tile()
+            for half in range(HALVES):
+                nc.scalar.activation(h[:, BANK * half : BANK * (half + 1)], x_banks[t][half][:], IDENTITY)
+            return h
+
+        lean_less_one = held([P, PACK], F32, "lean_less_one")
+        nc.scalar.activation(lean_less_one[:], lean_sb[:], COPY, bias=-1.0)
+
+        h_first = h_tile()
+        limit(0, h_first[:, 0:BANK], x_banks[0][0][:])
+        h_second = h_tile()
+        nc.scalar.activation(h_second[:, 0:BANK], x_banks[0][1][:], IDENTITY)
+        nc.vector.tensor_tensor(pages[0][:].indirect(bays[:, 0:LIST_COLS]), h_first[:, 0:BANK], wgs_of[0][:, 0:BANK], ALU.mult)
+        limit(0, h_second[:, 0:BANK], h_second[:, 0:BANK])
+        h = {1: evacuate(1)}
+        nc.vector.tensor_tensor(
+            pages[0][:].indirect(bays[:, LIST_COLS : 2 * LIST_COLS]), h_second[:, 0:BANK], wgs_of[0][:, BANK:S], ALU.mult
+        )
+
+        deck = [held([P, BANK, PACK], BF16, f"deck{c}") for c in range(CHUNKS)]
+
+        def round_page(t, c):
+            nc.scalar.copy(out=deck[c][:, :, t], in_=pages[t][:, BANK * c : BANK * (c + 1)])
+
+        for t in range(PACK):
+            port = ring.tile([P, PAIRS], F32, name="port", tag="port")
+            star = ring.tile([P, PAIRS], F32, name="star", tag="star")
+            rise = ring.tile([P, PAIRS], F32, name="rise", tag="rise")
+            nc.vector.tensor_copy(port[:], pages[t][:].indirect(ports[:]))
+            nc.vector.tensor_copy(star[:], pages[t][:].indirect(stars[:]))
+            if t + 1 < PACK:
+                limit(t + 1, h[t + 1][:], h[t + 1][:])
+            if t + 2 < PACK:
+                h[t + 2] = evacuate(t + 2)
+            if t == PACK - 2:
+                w5_grouped = ring.tile([P, PACK * N], BF16, name="grouped", tag="grouped", align_bytes=64)
+                nc.scalar.copy(
+                    out=w5_grouped[:].rearrange("p (c i j) -> p c j i", i=4, j=PACK),
+                    in_=w5_raw[:].rearrange("p j (c i) -> p c j i", i=4),
+                )
+                w5_codes, w5_scales = quantise(w5_grouped[:], "w5")
+            nc.vector.scalar_tensor_tensor(rise[:], port[:], lean_less_one[:, t : t + 1], star[:], ALU.mult, ALU.max)
+            nc.vector.tensor_tensor(pages[t][:].indirect(ports[:]), port[:], star[:], ALU.add)
+            if t + 1 < PACK:
+                nc.vector.tensor_tensor(pages[t + 1][:].indirect(bays[:]), h[t + 1][:], wgs_of[t + 1], ALU.mult)
+            nc.vector.tensor_tensor(pages[t][:].indirect(stars[:]), port[:], rise[:], ALU.add)
+            for c in range(CHUNKS):
+                round_page(t, c)
+
+        deck_mx = [quantise(deck[c][:].rearrange("p c t -> p (c t)"), f"deck{c}") for c in range(CHUNKS)]
+        for c in range(CHUNKS):
+            codes, scales = deck_mx[c]
+            for j in range(N // P):
+                rows = slice(P * j, P * (j + 1))
+                y4 = psum.tile([P, BANK], F32, name="bank", tag="bank")
+                nc.tensor.matmul_mx(
+                    out=y4[:],
+                    lhsT=w4_sb[:, 2 * P * j : 2 * P * (j + 1)].bitcast(FP4X4),
+                    lhsT_scale=w4_plane[:, rows],
+                    rhs=codes[:].bitcast(FP8X4),
+                    rhs_scale=scales[:],
+                    start=True,
+                    stop=True,
+                )
+                y5 = psum.tile([P, BANK], F32, name="bank", tag="bank")
+                nc.tensor.matmul_mx(
+                    out=y5[:],
+                    lhsT=w5_codes[:, rows].bitcast(FP8X4),
+                    lhsT_scale=w5_scales[:, rows],
+                    rhs=codes[:].bitcast(FP8X4),
+                    rhs_scale=scales[:],
+                    start=True,
+                    stop=True,
+                )
+                first = ring.tile([P, BANK], F32, name="first", tag="first", bufs=4)
+                if c == 0 and j < 2:
+                    nc.vector.tensor_scalar(first[:], y4[:], bias_sb[:, j : j + 1], None, ALU.add)
+                else:
+                    nc.scalar.activation(first[:], y4[:], IDENTITY, bias=bias_sb[:, j : j + 1])
+                result = ring.tile([P, BANK], F32, name="result", tag="result", bufs=6)
+                nc.vector.scalar_tensor_tensor(result[:], y5[:], bias_sb[:, j : j + 1], first[:], ALU.add, ALU.max)
+                nc.sync.dma_start(out=out[rows, BANK * c : BANK * (c + 1)], in_=result[:])

@@ -26,6 +26,11 @@ HALVES = S // BANK
 CHUNKS = T2 // BANK
 QUAD = 32
 LIST_COLS = BANK // 16
+HALF_P = P // 2
+HALF_H = H // 2
+LOW, HIGH = slice(0, HALF_P), slice(HALF_P, P)
+PAGES = 4
+ODD_BYTE = {2: 3, 3: 1}
 
 
 def tile_list_ferry_bay_marshalling_kernel(
@@ -37,22 +42,30 @@ def tile_list_ferry_bay_marshalling_kernel(
         ring = ctx.enter_context(tc.tile_pool(name="ring", bufs=2))
         psum = ctx.enter_context(tc.psum_pool(name="psum", bufs=8))
 
-        def held(shape, dtype, name):
-            return keep.tile(shape, dtype, name=name, align_bytes=64)
+        def held(shape, dtype, name, tag=""):
+            return keep.tile(shape, dtype, name=name, tag=tag or name, align_bytes=64)
 
         def load_list(src, name):
             t = keep.tile(list(src.shape), U16, name=name)
             nc.sync.dma_start(t[:], src)
             return t
 
-        def load_rows(vec, name):
-            t = held([P, PACK], F32, name)
-            nc.sync.dma_start(out=t[:], in_=vec.rearrange("(p t) -> p t", t=PACK))
-            return t
+        def load_even_rows(vec, g, name):
+            t = held([P, 1], F32, name)
+            with nc.allow_non_contiguous_dma(reason="one value to a partition"):
+                nc.sync.dma_start(out=t[:], in_=vec.rearrange("(g p o) -> g p o", g=2, o=2)[g, :, 0:1])
+            return t[:, 0:1]
 
-        def load_weight(rows):
-            raw = ring.tile([P, PACK, H], F32, name="raw", tag="raw", bufs=3, align_bytes=64)
-            nc.sync.dma_start(out=raw[:], in_=rows.rearrange("(p j) c -> p j c", j=PACK))
+        def load_odd_rows(vec, name):
+            t = held([P, PACK], F32, name)
+            nc.sync.dma_start(out=t[:], in_=vec.rearrange("(p b) -> p b", b=PACK))
+            return [t[:, ODD_BYTE[g] : ODD_BYTE[g] + 1] for g in (2, 3)]
+
+        def load_weight(rows, half):
+            raw = ring.tile([P, PACK, HALF_H], F32, name="raw", tag="raw", bufs=2 * PASSES, align_bytes=64)
+            nc.sync.dma_start(
+                out=raw[:], in_=rows[:, HALF_H * half : HALF_H * (half + 1)].rearrange("(p j) c -> p j c", j=PACK)
+            )
             return raw
 
         def load_table(a):
@@ -60,21 +73,18 @@ def tile_list_ferry_bay_marshalling_kernel(
             nc.sync.dma_start(out=t[:], in_=tab_words[a].rearrange("p t i -> p (t i)").bitcast(I32))
             return t
 
-        def load_page(t):
-            pg = held([P, T2], F32, f"page{t}")
-            nc.sync.dma_start(out=pg[:], in_=page0.rearrange("(p t) c -> t p c", t=PACK)[t])
+        def load_page(g):
+            pg = held([P, T2], F32, f"page{g}")
+            if g < 2:
+                nc.sync.dma_start(out=pg[:], in_=page0.rearrange("(g p o) c -> g o p c", g=2, o=2)[g, 0])
+            else:
+                nc.sync.dma_start(out=pg[:], in_=page0.rearrange("(p b) c -> b p c", b=PACK)[ODD_BYTE[g]])
             return pg
 
-        def load_wgs(t0, t1, name):
-            w = held([P, t1 - t0, S], F32, name)
-            src = wgs.rearrange("(q t) j -> q t j", t=PACK)[:, t0:t1, :]
-            for q in range(P // QUAD):
-                nc.sync.dma_start(out=w[QUAD * q : QUAD * (q + 1), :, :], in_=src)
-            return w
-
         def quantise(grouped, name):
-            codes = held([P, BANK], U32, name + "_codes")
-            scales = held([P, BANK], U8, name + "_scales")
+            width = grouped.shape[1] // PACK
+            codes = held([P, width], U32, name + "_codes")
+            scales = held([P, width], U8, name + "_scales")
             nc.vector.quantize_mx(out=codes[:].bitcast(FP8X4), scales=scales[:], in_=grouped)
             return codes, scales
 
@@ -83,6 +93,7 @@ def tile_list_ferry_bay_marshalling_kernel(
         w4_plane = held([P, N], U8, "w4_plane")
         nc.vector.memset(w4_plane[:].bitcast(I32), 0)
 
+        w1_rows = [w1[K_PASS * a : K_PASS * (a + 1), :] for a in range(PASSES)]
         picks = load_list(offs, "picks")
         table = [load_table(0)]
         for q in range(P // QUAD):
@@ -90,59 +101,137 @@ def tile_list_ferry_bay_marshalling_kernel(
                 out=table_scales[QUAD * q : QUAD * q + 4 * PASSES, :].bitcast(I32),
                 in_=tab_scales[:, 4 * q : 4 * q + 4, :].bitcast(I32),
             )
-        w1_raw = [load_weight(w1[0:K_PASS, :])]
+        w1_low = [load_weight(w1_rows[0], 0)]
         table.append(load_table(1))
-        w1_raw.append(load_weight(w1[K_PASS : 2 * K_PASS, :]))
-        w1_raw.append(load_weight(w1[2 * K_PASS : 3 * K_PASS, :]))
-        cap_sb = load_rows(cap, "cap")
-        gain_sb = load_rows(gain, "gain")
+        w1_low += [load_weight(w1_rows[a], 0) for a in range(1, PASSES)]
+        cap_of = [load_even_rows(cap, 0, "cap0")]
+        gain_of = [load_even_rows(gain, 0, "gain0")]
         table.append(load_table(2))
         bays = load_list(offs2, "bays")
-        wgs_first = load_wgs(0, 1, "wgs_first")
+        wgs_even = held([P, S], F32, "wgs_even")
+
+        def load_wgs_even(half):
+            cols = slice(BANK * half, BANK * (half + 1))
+            for part in (LOW, HIGH):
+                nc.sync.dma_start(out=wgs_even[part, cols], in_=wgs.rearrange("(q o) j -> o q j", o=2)[0, :, cols])
+
+        load_wgs_even(0)
         pages = [load_page(0)]
+        w1_high = [load_weight(w1_rows[0], 1)]
+        load_wgs_even(1)
+        w1_high += [load_weight(w1_rows[a], 1) for a in range(1, PASSES)]
         ports = load_list(offs3, "ports")
         stars = load_list(offs4, "stars")
-        lean_sb = load_rows(lean, "lean")
+        lean_of = [load_even_rows(lean, 0, "lean0")]
+        cap_of.append(load_even_rows(cap, 1, "cap1"))
+        gain_of.append(load_even_rows(gain, 1, "gain1"))
         pages.append(load_page(1))
-        wgs_rest = load_wgs(1, PACK, "wgs_rest")
+        lean_of.append(load_even_rows(lean, 1, "lean1"))
+        cap_of += load_odd_rows(cap, "cap_odd")
+        gain_of += load_odd_rows(gain, "gain_odd")
+        lean_of += load_odd_rows(lean, "lean_odd")
+        wgs_odd = held([P, 2, S], F32, "wgs_odd")
+        for q in range(P // QUAD):
+            nc.sync.dma_start(
+                out=wgs_odd[QUAD * q : QUAD * (q + 1), :, :], in_=wgs.rearrange("(q e o) j -> o q e j", e=2, o=2)[1]
+            )
         pages.append(load_page(2))
         pages.append(load_page(3))
-        wgs_of = [wgs_first[:, 0, :]] + [wgs_rest[:, t, :] for t in range(PACK - 1)]
+        wgs_of = [wgs_even[:], wgs_even[:], wgs_odd[:, 1, :], wgs_odd[:, 0, :]]
 
         picked = [held([P, S], U32, f"picked{a}") for a in range(PASSES)]
         picked_scales = held([P, S], U8, "picked_scales")
-        x_banks = [[psum.tile([P, BANK], F32, name="bank", tag="bank") for half in range(HALVES)] for t in range(PACK)]
+        x_banks = [[psum.tile([P, BANK], F32, name="bank", tag="bank") for half in range(HALVES)] for g in range(PAGES)]
+
+        def first_product(a, g, half, codes, scales, slot):
+            rows = slice(P * slot, P * (slot + 1))
+            cols = slice(BANK * half, BANK * (half + 1))
+            nc.tensor.matmul_mx(
+                out=x_banks[g][half][:],
+                lhsT=codes[:, rows].bitcast(FP8X4),
+                lhsT_scale=scales[:, rows],
+                rhs=picked[a][:, cols].bitcast(FP8X4),
+                rhs_scale=picked_scales[4 * a : P, cols],
+                start=(a == 0),
+                stop=(a == PASSES - 1),
+            )
+
+        def group_even(dst, raw):
+            nc.scalar.copy(
+                out=dst.rearrange("p (q u j) -> p q j u", u=2, j=PACK),
+                in_=raw[:].rearrange("p j (q u o) -> p q j u o", u=2, o=2)[:, :, :, :, 0],
+            )
+
+        def group_odd(dst, raw, half):
+            nc.scalar.copy(
+                out=dst.rearrange("p (e h q j) -> p h q j e", e=2, h=2, j=PACK)[:, half],
+                in_=raw[:].rearrange("p j (q e o) -> p q j e o", e=2, o=2)[:, :, :, :, 1],
+            )
+
+        grouped_second = held([P, PASSES * K_PASS], BF16, "grouped_second")
+        grouped_odd = held([P, PASSES, 2 * K_PASS], BF16, "grouped_odd")
         for a in range(PASSES):
             window = table[a][:].bitcast(U32)
             if a < PASSES - 1:
                 nc.vector.tensor_copy(picked[a][:], window.indirect(picks[:]))
             if a == 0:
                 nc.vector.tensor_copy(picked_scales[:], table_scales[:].indirect(picks[:]))
-            grouped = ring.tile([P, PACK * H], BF16, name="grouped", tag="grouped", align_bytes=64)
-            nc.scalar.copy(
-                out=grouped[:].rearrange("p (t m j) -> p m j t", t=PACK, j=PACK),
-                in_=w1_raw[a][:].rearrange("p j (m t) -> p m j t", t=PACK),
-            )
-            w1_codes, w1_scales = quantise(grouped[:], f"w1_{a}")
+            grouped = held([P, K_PASS], BF16, f"grouped_first{a}")
+            group_even(grouped[:], w1_low[a])
+            codes, scales = quantise(grouped[:], f"w1_first{a}")
+            group_odd(grouped_odd[:, a, :], w1_low[a], 0)
             for half in range(HALVES):
-                cols = slice(BANK * half, BANK * (half + 1))
                 if a == PASSES - 1:
                     nc.vector.tensor_copy(
-                        picked[a][:, cols], window.indirect(picks[:, LIST_COLS * half : LIST_COLS * (half + 1)])
+                        picked[a][:, BANK * half : BANK * (half + 1)],
+                        window.indirect(picks[:, LIST_COLS * half : LIST_COLS * (half + 1)]),
                     )
-                for t in range(PACK):
-                    rows = slice(P * t, P * (t + 1))
-                    nc.tensor.matmul_mx(
-                        out=x_banks[t][half][:],
-                        lhsT=w1_codes[:, rows].bitcast(FP8X4),
-                        lhsT_scale=w1_scales[:, rows],
-                        rhs=picked[a][:, cols].bitcast(FP8X4),
-                        rhs_scale=picked_scales[4 * a : P, cols],
-                        start=(a == 0),
-                        stop=(a == PASSES - 1),
-                    )
+                first_product(a, 0, half, codes, scales, 0)
 
-        w5_raw = load_weight(w5)
+        def h_tile():
+            return ring.tile([P, S], F32, name="h", tag="h")
+
+        def limit(g, dst, src):
+            nc.vector.tensor_scalar(dst, src, cap_of[g], gain_of[g], ALU.min, ALU.mult)
+
+        def evacuate(g):
+            h = h_tile()
+            for half in range(HALVES):
+                nc.scalar.activation(h[:, BANK * half : BANK * (half + 1)], x_banks[g][half][:], IDENTITY)
+            return h
+
+        h_first = h_tile()
+        limit(0, h_first[:, 0:BANK], x_banks[0][0][:])
+        h_second = h_tile()
+        nc.scalar.activation(h_second[:, 0:BANK], x_banks[0][1][:], IDENTITY)
+        nc.vector.tensor_tensor(pages[0][:].indirect(bays[:, 0:LIST_COLS]), h_first[:, 0:BANK], wgs_of[0][:, 0:BANK], ALU.mult)
+        limit(0, h_second[:, 0:BANK], h_second[:, 0:BANK])
+        nc.vector.tensor_tensor(
+            pages[0][:].indirect(bays[:, LIST_COLS : 2 * LIST_COLS]), h_second[:, 0:BANK], wgs_of[0][:, BANK:S], ALU.mult
+        )
+
+        lean_less_one = held([P, PAGES], F32, "lean_less_one")
+        for g in range(PAGES):
+            nc.scalar.activation(lean_less_one[:, g : g + 1], lean_of[g], COPY, bias=-1.0)
+
+        for a in range(PASSES):
+            group_even(grouped_second[:, K_PASS * a : K_PASS * (a + 1)], w1_high[a])
+        codes, scales = quantise(grouped_second[:], "w1_second")
+        for half in range(HALVES):
+            for a in range(PASSES):
+                first_product(a, 1, half, codes, scales, a)
+        for a in range(PASSES):
+            group_odd(grouped_odd[:, a, :], w1_high[a], 1)
+        odd_front = quantise(grouped_odd[:, 0:2, :].rearrange("p a c -> p (a c)"), "w1_odd_front")
+        odd_back = quantise(grouped_odd[:, 2, :], "w1_odd_back")
+        for g, slot in ((2, 1), (3, 0)):
+            for half in range(HALVES):
+                for a in range(PASSES):
+                    codes, scales = odd_front if a < 2 else odd_back
+                    first_product(a, g, half, codes, scales, 2 * (a % 2) + slot)
+        h = {1: evacuate(1)}
+
+        w5_raw = [load_weight(w5, half) for half in range(2)]
         w4_sb = held([P, 2 * N], U8, "w4")
         nc.sync.dma_start(out=w4_sb[:].bitcast(I32), in_=w4_words[0].bitcast(I32))
         for q in range(P // QUAD):
@@ -154,61 +243,55 @@ def tile_list_ferry_bay_marshalling_kernel(
         with nc.allow_non_contiguous_dma(reason="one bias value to a partition"):
             nc.sync.dma_start(out=bias_sb[:], in_=bias.rearrange("(j p) -> p j", p=P))
 
-        def h_tile():
-            return ring.tile([P, S], F32, name="h", tag="h")
-
-        def limit(t, dst, src):
-            nc.vector.tensor_scalar(dst, src, cap_sb[:, t : t + 1], gain_sb[:, t : t + 1], ALU.min, ALU.mult)
-
-        def evacuate(t):
-            h = h_tile()
-            for half in range(HALVES):
-                nc.scalar.activation(h[:, BANK * half : BANK * (half + 1)], x_banks[t][half][:], IDENTITY)
-            return h
-
-        lean_less_one = held([P, PACK], F32, "lean_less_one")
-        nc.scalar.activation(lean_less_one[:], lean_sb[:], COPY, bias=-1.0)
-
-        h_first = h_tile()
-        limit(0, h_first[:, 0:BANK], x_banks[0][0][:])
-        h_second = h_tile()
-        nc.scalar.activation(h_second[:, 0:BANK], x_banks[0][1][:], IDENTITY)
-        nc.vector.tensor_tensor(pages[0][:].indirect(bays[:, 0:LIST_COLS]), h_first[:, 0:BANK], wgs_of[0][:, 0:BANK], ALU.mult)
-        limit(0, h_second[:, 0:BANK], h_second[:, 0:BANK])
-        h = {1: evacuate(1)}
-        nc.vector.tensor_tensor(
-            pages[0][:].indirect(bays[:, LIST_COLS : 2 * LIST_COLS]), h_second[:, 0:BANK], wgs_of[0][:, BANK:S], ALU.mult
-        )
-
         deck = [held([P, BANK, PACK], BF16, f"deck{c}") for c in range(CHUNKS)]
+        moved = held([P, 2, T2], F32, "moved")
 
-        def round_page(t, c):
-            nc.scalar.copy(out=deck[c][:, :, t], in_=pages[t][:, BANK * c : BANK * (c + 1)])
-
-        for t in range(PACK):
-            port = ring.tile([P, PAIRS], F32, name="port", tag="port")
-            star = ring.tile([P, PAIRS], F32, name="star", tag="star")
-            rise = ring.tile([P, PAIRS], F32, name="rise", tag="rise")
-            nc.vector.tensor_copy(port[:], pages[t][:].indirect(ports[:]))
-            nc.vector.tensor_copy(star[:], pages[t][:].indirect(stars[:]))
-            if t + 1 < PACK:
-                limit(t + 1, h[t + 1][:], h[t + 1][:])
-            if t + 2 < PACK:
-                h[t + 2] = evacuate(t + 2)
-            if t == PACK - 2:
-                w5_grouped = ring.tile([P, PACK * N], BF16, name="grouped", tag="grouped", align_bytes=64)
-                nc.scalar.copy(
-                    out=w5_grouped[:].rearrange("p (c i j) -> p c j i", i=4, j=PACK),
-                    in_=w5_raw[:].rearrange("p j (c i) -> p c j i", i=4),
-                )
-                w5_codes, w5_scales = quantise(w5_grouped[:], "w5")
-            nc.vector.scalar_tensor_tensor(rise[:], port[:], lean_less_one[:, t : t + 1], star[:], ALU.mult, ALU.max)
-            nc.vector.tensor_tensor(pages[t][:].indirect(ports[:]), port[:], star[:], ALU.add)
-            if t + 1 < PACK:
-                nc.vector.tensor_tensor(pages[t + 1][:].indirect(bays[:]), h[t + 1][:], wgs_of[t + 1], ALU.mult)
-            nc.vector.tensor_tensor(pages[t][:].indirect(stars[:]), port[:], rise[:], ALU.add)
+        def round_rows(src, byte, on_vector=()):
             for c in range(CHUNKS):
-                round_page(t, c)
+                dst, cols = deck[c][:, :, byte], src[:, BANK * c : BANK * (c + 1)]
+                if c in on_vector:
+                    nc.vector.tensor_copy(out=dst, in_=cols)
+                else:
+                    nc.scalar.copy(out=dst, in_=cols)
+
+        for g in range(PAGES):
+            if g == 0:
+                port = held([P, PAIRS], F32, "port_first", tag="grouped_second")[:]
+                star, rise = [ring.tile([P, PAIRS], F32, name=n, tag=n)[:] for n in ("star", "rise")]
+            elif g == PAGES - 1:
+                last = held([P, 3, PAIRS], F32, "pair_last", tag="moved")
+                port, star, rise = last[:, 0, :], last[:, 1, :], last[:, 2, :]
+            else:
+                port, star, rise = [ring.tile([P, PAIRS], F32, name=n, tag=n)[:] for n in ("port", "star", "rise")]
+            nc.vector.tensor_copy(port, pages[g][:].indirect(ports[:]))
+            nc.vector.tensor_copy(star, pages[g][:].indirect(stars[:]))
+            if g + 1 < PAGES:
+                limit(g + 1, h[g + 1][:], h[g + 1][:])
+            if g + 2 < PAGES:
+                h[g + 2] = evacuate(g + 2)
+            if g == 1:
+                w5_grouped = held([P, PACK * N], BF16, "w5_grouped")
+                for half in range(2):
+                    nc.scalar.copy(
+                        out=w5_grouped[:, 2 * N * half : 2 * N * (half + 1)].rearrange("p (c i j) -> p c j i", i=4, j=PACK),
+                        in_=w5_raw[half][:].rearrange("p j (c i) -> p c j i", i=4),
+                    )
+                w5_codes, w5_scales = quantise(w5_grouped[:], "w5")
+            nc.vector.scalar_tensor_tensor(rise, port, lean_less_one[:, g : g + 1], star, ALU.mult, ALU.max)
+            nc.vector.tensor_tensor(pages[g][:].indirect(ports[:]), port, star, ALU.add)
+            if g + 1 < PAGES:
+                nc.vector.tensor_tensor(pages[g + 1][:].indirect(bays[:]), h[g + 1][:], wgs_of[g + 1], ALU.mult)
+            nc.vector.tensor_tensor(pages[g][:].indirect(stars[:]), port, rise, ALU.add)
+            if g < 2:
+                nc.scalar.dma_start(out=moved[(LOW, HIGH)[g], :, :], in_=pages[g][:])
+            if g == 1:
+                for c in range(CHUNKS):
+                    nc.scalar.copy(
+                        out=deck[c][:].rearrange("p c (u o) -> p c u o", o=2)[:, :, :, 0],
+                        in_=moved[:, :, BANK * c : BANK * (c + 1)].rearrange("p u c -> p c u"),
+                    )
+            if g >= 2:
+                round_rows(pages[g], ODD_BYTE[g], on_vector=(0, CHUNKS - 1) if g == PAGES - 1 else ())
 
         deck_mx = [quantise(deck[c][:].rearrange("p c t -> p (c t)"), f"deck{c}") for c in range(CHUNKS)]
         for c in range(CHUNKS):
@@ -236,10 +319,7 @@ def tile_list_ferry_bay_marshalling_kernel(
                     stop=True,
                 )
                 first = ring.tile([P, BANK], F32, name="first", tag="first", bufs=4)
-                if c == 0 and j < 2:
-                    nc.vector.tensor_scalar(first[:], y4[:], bias_sb[:, j : j + 1], None, ALU.add)
-                else:
-                    nc.scalar.activation(first[:], y4[:], IDENTITY, bias=bias_sb[:, j : j + 1])
-                result = ring.tile([P, BANK], F32, name="result", tag="result", bufs=6)
+                nc.scalar.activation(first[:], y4[:], IDENTITY, bias=bias_sb[:, j : j + 1])
+                result = ring.tile([P, BANK], F32, name="result", tag="raw", bufs=2 * PASSES, align_bytes=64)
                 nc.vector.scalar_tensor_tensor(result[:], y5[:], bias_sb[:, j : j + 1], first[:], ALU.add, ALU.max)
                 nc.sync.dma_start(out=out[rows, BANK * c : BANK * (c + 1)], in_=result[:])

@@ -28,7 +28,6 @@ QUAD = 32
 LIST_COLS = BANK // 16
 HALF_P = P // 2
 HALF_H = H // 2
-LOW, HIGH = slice(0, HALF_P), slice(HALF_P, P)
 PAGES = 4
 ODD_BYTE = {2: 3, 3: 1}
 
@@ -53,7 +52,7 @@ def tile_list_ferry_bay_marshalling_kernel(
         def load_even_rows(vec, g, name):
             t = held([P, 1], F32, name)
             with nc.allow_non_contiguous_dma(reason="one value to a partition"):
-                nc.sync.dma_start(out=t[:], in_=vec.rearrange("(g p o) -> g p o", g=2, o=2)[g, :, 0:1])
+                nc.sync.dma_start(out=t[:], in_=vec.rearrange("(g h m o) -> g m h o", g=2, h=2, o=2)[g, :, :, 0:1])
             return t[:, 0:1]
 
         def load_odd_rows(vec, name):
@@ -76,7 +75,7 @@ def tile_list_ferry_bay_marshalling_kernel(
         def load_page(g):
             pg = held([P, T2], F32, f"page{g}")
             if g < 2:
-                nc.sync.dma_start(out=pg[:], in_=page0.rearrange("(g p o) c -> g o p c", g=2, o=2)[g, 0])
+                nc.sync.dma_start(out=pg[:], in_=page0.rearrange("(g h m o) c -> g o m h c", g=2, h=2, o=2)[g, 0])
             else:
                 nc.sync.dma_start(out=pg[:], in_=page0.rearrange("(p b) c -> b p c", b=PACK)[ODD_BYTE[g]])
             return pg
@@ -97,7 +96,7 @@ def tile_list_ferry_bay_marshalling_kernel(
         picks = load_list(offs, "picks")
         table = [load_table(0)]
         for q in range(P // QUAD):
-            nc.sync.dma_start(
+            nc.gpsimd.dma_start(
                 out=table_scales[QUAD * q : QUAD * q + 4 * PASSES, :].bitcast(I32),
                 in_=tab_scales[:, 4 * q : 4 * q + 4, :].bitcast(I32),
             )
@@ -112,14 +111,13 @@ def tile_list_ferry_bay_marshalling_kernel(
 
         def load_wgs_even(half):
             cols = slice(BANK * half, BANK * (half + 1))
-            for part in (LOW, HIGH):
-                nc.sync.dma_start(out=wgs_even[part, cols], in_=wgs.rearrange("(q o) j -> o q j", o=2)[0, :, cols])
+            rows = wgs.rearrange("(m o) j -> m o j", o=2)[:, 0:1, cols]
+            nc.sync.dma_start(out=wgs_even[:, cols], in_=rows.to_broadcast([HALF_P, 2, BANK]))
 
         load_wgs_even(0)
         pages = [load_page(0)]
-        w1_high = [load_weight(w1_rows[0], 1)]
         load_wgs_even(1)
-        w1_high += [load_weight(w1_rows[a], 1) for a in range(1, PASSES)]
+        w1_high = [load_weight(w1_rows[a], 1) for a in range(PASSES)]
         ports = load_list(offs3, "ports")
         stars = load_list(offs4, "stars")
         lean_of = [load_even_rows(lean, 0, "lean0")]
@@ -139,7 +137,7 @@ def tile_list_ferry_bay_marshalling_kernel(
         pages.append(load_page(3))
         wgs_of = [wgs_even[:], wgs_even[:], wgs_odd[:, 1, :], wgs_odd[:, 0, :]]
 
-        picked = [held([P, S], U32, f"picked{a}") for a in range(PASSES)]
+        picked = [held([P, S], U32, f"picked{a}") for a in range(PASSES - 1)]
         picked_scales = held([P, S], U8, "picked_scales")
         x_banks = [[psum.tile([P, BANK], F32, name="bank", tag="bank") for half in range(HALVES)] for g in range(PAGES)]
 
@@ -158,8 +156,8 @@ def tile_list_ferry_bay_marshalling_kernel(
 
         def group_even(dst, raw):
             nc.scalar.copy(
-                out=dst.rearrange("p (q u j) -> p q j u", u=2, j=PACK),
-                in_=raw[:].rearrange("p j (q u o) -> p q j u o", u=2, o=2)[:, :, :, :, 0],
+                out=dst.rearrange("p (m i h j) -> p m h j i", i=2, h=2, j=PACK),
+                in_=raw[:].rearrange("p j (h m i o) -> p m h j i o", h=2, i=2, o=2)[:, :, :, :, :, 0],
             )
 
         def group_odd(dst, raw, half):
@@ -180,6 +178,8 @@ def tile_list_ferry_bay_marshalling_kernel(
             group_even(grouped[:], w1_low[a])
             codes, scales = quantise(grouped[:], f"w1_first{a}")
             group_odd(grouped_odd[:, a, :], w1_low[a], 0)
+            if a == PASSES - 1:
+                picked.append(held([P, S], U32, f"picked{a}", tag="table_scales"))
             for half in range(HALVES):
                 if a == PASSES - 1:
                     nc.vector.tensor_copy(
@@ -244,7 +244,7 @@ def tile_list_ferry_bay_marshalling_kernel(
             nc.sync.dma_start(out=bias_sb[:], in_=bias.rearrange("(j p) -> p j", p=P))
 
         deck = [held([P, BANK, PACK], BF16, f"deck{c}") for c in range(CHUNKS)]
-        moved = held([P, 2, T2], F32, "moved")
+        moved = [held([P, 2, T2 // 2], F32, f"moved{half}") for half in range(2)]
 
         def round_rows(src, byte, on_vector=()):
             for c in range(CHUNKS):
@@ -259,8 +259,9 @@ def tile_list_ferry_bay_marshalling_kernel(
                 port = held([P, PAIRS], F32, "port_first", tag="grouped_second")[:]
                 star, rise = [ring.tile([P, PAIRS], F32, name=n, tag=n)[:] for n in ("star", "rise")]
             elif g == PAGES - 1:
-                last = held([P, 3, PAIRS], F32, "pair_last", tag="moved")
-                port, star, rise = last[:, 0, :], last[:, 1, :], last[:, 2, :]
+                port = held([P, PAIRS], F32, "port_last", tag="moved0")[:]
+                last = held([P, 2, PAIRS], F32, "pair_last", tag="moved1")
+                star, rise = last[:, 0, :], last[:, 1, :]
             else:
                 port, star, rise = [ring.tile([P, PAIRS], F32, name=n, tag=n)[:] for n in ("port", "star", "rise")]
             nc.vector.tensor_copy(port, pages[g][:].indirect(ports[:]))
@@ -283,12 +284,16 @@ def tile_list_ferry_bay_marshalling_kernel(
                 nc.vector.tensor_tensor(pages[g + 1][:].indirect(bays[:]), h[g + 1][:], wgs_of[g + 1], ALU.mult)
             nc.vector.tensor_tensor(pages[g][:].indirect(stars[:]), port, rise, ALU.add)
             if g < 2:
-                nc.scalar.dma_start(out=moved[(LOW, HIGH)[g], :, :], in_=pages[g][:])
+                for half in range(2):
+                    cols = slice(T2 // 2 * half, T2 // 2 * (half + 1))
+                    for low in range(2):
+                        first_row = QUAD * (2 * g + low)
+                        nc.scalar.dma_start(out=moved[half][first_row : first_row + QUAD, :, :], in_=pages[g][low:P:2, cols])
             if g == 1:
                 for c in range(CHUNKS):
                     nc.scalar.copy(
                         out=deck[c][:].rearrange("p c (u o) -> p c u o", o=2)[:, :, :, 0],
-                        in_=moved[:, :, BANK * c : BANK * (c + 1)].rearrange("p u c -> p c u"),
+                        in_=moved[c // 2][:, :, BANK * (c % 2) : BANK * (c % 2 + 1)].rearrange("p u c -> p c u"),
                     )
             if g >= 2:
                 round_rows(pages[g], ODD_BYTE[g], on_vector=(0, CHUNKS - 1) if g == PAGES - 1 else ())

@@ -93,8 +93,8 @@ def tile_list_ferry_bay_marshalling_kernel(
         nc.vector.memset(w4_plane[:].bitcast(I32), 0)
 
         w1_rows = [w1[K_PASS * a : K_PASS * (a + 1), :] for a in range(PASSES)]
-        picks = load_list(offs, "picks")
         table = [load_table(0)]
+        picks = load_list(offs, "picks")
         for q in range(P // QUAD):
             nc.gpsimd.dma_start(
                 out=table_scales[QUAD * q : QUAD * q + 4 * PASSES, :].bitcast(I32),
@@ -243,16 +243,21 @@ def tile_list_ferry_bay_marshalling_kernel(
         with nc.allow_non_contiguous_dma(reason="one bias value to a partition"):
             nc.sync.dma_start(out=bias_sb[:], in_=bias.rearrange("(j p) -> p j", p=P))
 
+        w5_grouped = held([P, PACK * N], BF16, "w5_grouped")
         deck = [held([P, BANK, PACK], BF16, f"deck{c}") for c in range(CHUNKS)]
         moved = [held([P, 2, T2 // 2], F32, f"moved{half}") for half in range(2)]
 
-        def round_rows(src, byte, on_vector=()):
-            for c in range(CHUNKS):
-                dst, cols = deck[c][:, :, byte], src[:, BANK * c : BANK * (c + 1)]
-                if c in on_vector:
-                    nc.vector.tensor_copy(out=dst, in_=cols)
-                else:
-                    nc.scalar.copy(out=dst, in_=cols)
+        def round_rows(copy, g, c):
+            copy(out=deck[c][:, :, ODD_BYTE[g]], in_=pages[g][:, BANK * c : BANK * (c + 1)])
+
+        w5_mx = []
+
+        def quantise_w5():
+            j = len(w5_mx)
+            w5_mx.append(quantise(w5_grouped[:, K_PASS * j : K_PASS * (j + 1)], f"w5_{j}"))
+
+        def quantise_deck(c):
+            return quantise(deck[c][:].rearrange("p c t -> p (c t)"), f"deck{c}")
 
         for g in range(PAGES):
             if g == 0:
@@ -271,17 +276,19 @@ def tile_list_ferry_bay_marshalling_kernel(
             if g + 2 < PAGES:
                 h[g + 2] = evacuate(g + 2)
             if g == 1:
-                w5_grouped = held([P, PACK * N], BF16, "w5_grouped")
                 for half in range(2):
                     nc.scalar.copy(
                         out=w5_grouped[:, 2 * N * half : 2 * N * (half + 1)].rearrange("p (c i j) -> p c j i", i=4, j=PACK),
                         in_=w5_raw[half][:].rearrange("p j (c i) -> p c j i", i=4),
                     )
-                w5_codes, w5_scales = quantise(w5_grouped[:], "w5")
+            if g == PAGES - 1:
+                quantise_w5()
             nc.vector.scalar_tensor_tensor(rise, port, lean_less_one[:, g : g + 1], star, ALU.mult, ALU.max)
             nc.vector.tensor_tensor(pages[g][:].indirect(ports[:]), port, star, ALU.add)
             if g + 1 < PAGES:
                 nc.vector.tensor_tensor(pages[g + 1][:].indirect(bays[:]), h[g + 1][:], wgs_of[g + 1], ALU.mult)
+            else:
+                quantise_w5()
             nc.vector.tensor_tensor(pages[g][:].indirect(stars[:]), port, rise, ALU.add)
             if g < 2:
                 for half in range(2):
@@ -295,10 +302,18 @@ def tile_list_ferry_bay_marshalling_kernel(
                         out=deck[c][:].rearrange("p c (u o) -> p c u o", o=2)[:, :, :, 0],
                         in_=moved[c // 2][:, :, BANK * (c % 2) : BANK * (c % 2 + 1)].rearrange("p u c -> p c u"),
                     )
-            if g >= 2:
-                round_rows(pages[g], ODD_BYTE[g], on_vector=(0, CHUNKS - 1) if g == PAGES - 1 else ())
+            if g == 2:
+                for c in range(CHUNKS):
+                    round_rows(nc.scalar.copy, g, c)
 
-        deck_mx = [quantise(deck[c][:].rearrange("p c t -> p (c t)"), f"deck{c}") for c in range(CHUNKS)]
+        quantise_w5()
+        round_rows(nc.vector.tensor_copy, PAGES - 1, 0)
+        for c in range(1, CHUNKS - 1):
+            round_rows(nc.scalar.copy, PAGES - 1, c)
+        quantise_w5()
+        deck_mx = [quantise_deck(0)]
+        round_rows(nc.vector.tensor_copy, PAGES - 1, CHUNKS - 1)
+        deck_mx += [quantise_deck(c) for c in range(1, CHUNKS)]
         for c in range(CHUNKS):
             codes, scales = deck_mx[c]
             for j in range(N // P):
@@ -316,8 +331,8 @@ def tile_list_ferry_bay_marshalling_kernel(
                 y5 = psum.tile([P, BANK], F32, name="bank", tag="bank")
                 nc.tensor.matmul_mx(
                     out=y5[:],
-                    lhsT=w5_codes[:, rows].bitcast(FP8X4),
-                    lhsT_scale=w5_scales[:, rows],
+                    lhsT=w5_mx[j][0][:].bitcast(FP8X4),
+                    lhsT_scale=w5_mx[j][1][:],
                     rhs=codes[:].bitcast(FP8X4),
                     rhs_scale=scales[:],
                     start=True,

from contextlib import ExitStack

import concourse.mybir as mybir

K, H, N, T, S, T2, PAIRS = 1536, 512, 512, 4096, 1024, 2048, 512
FLOPS = 2 * K * H * S + 2 * 2 * H * N * T2

F32 = mybir.dt.float32
BF16 = mybir.dt.bfloat16
I32 = mybir.dt.int32
U32 = mybir.dt.uint32
U16 = mybir.dt.uint16
U8 = mybir.dt.uint8
FP8X4 = mybir.dt.float8_e4m3fn_x4
FP4X4 = mybir.dt.float4_e2m1fn_x4
ALU = mybir.AluOpType
COPY = mybir.ActivationFunctionType.Copy
IDENTITY = mybir.ActivationFunctionType.Identity

P = 128
PACK = 4
K_PASS = P * PACK
PASSES = K // K_PASS
BANK = 512
HALVES = S // BANK
CHUNKS = T2 // BANK
QUAD = 32
LIST_COLS = BANK // 16
HALF_P = P // 2
HALF_H = H // 2
PAGES = 4
ODD_BYTE = {2: 3, 3: 1}


def tile_list_ferry_bay_marshalling_kernel(
    tc, tab_words, tab_scales, offs, offs2, offs3, offs4, w1, cap, gain, wgs, page0, lean, w4_words, w4_scales, w5, bias, out
):
    nc = tc.nc
    with ExitStack() as ctx:
        keep = ctx.enter_context(tc.tile_pool(name="keep", bufs=1))
        ring = ctx.enter_context(tc.tile_pool(name="ring", bufs=2))
        psum = ctx.enter_context(tc.psum_pool(name="psum", bufs=8))

        def held(shape, dtype, name, tag=""):
            return keep.tile(shape, dtype, name=name, tag=tag or name, align_bytes=64)

        def load_list(src, name):
            t = keep.tile(list(src.shape), U16, name=name)
            nc.sync.dma_start(t[:], src)
            return t

        def load_even_rows(vec, g, name):
            t = held([P, 1], F32, name)
            with nc.allow_non_contiguous_dma(reason="one value to a partition"):
                nc.sync.dma_start(out=t[:], in_=vec.rearrange("(g h m o) -> g m h o", g=2, h=2, o=2)[g, :, :, 0:1])
            return t[:, 0:1]

        def load_odd_rows(vec, name):
            t = held([P, PACK], F32, name)
            nc.sync.dma_start(out=t[:], in_=vec.rearrange("(p b) -> p b", b=PACK))
            return [t[:, ODD_BYTE[g] : ODD_BYTE[g] + 1] for g in (2, 3)]

        def load_weight(rows, half):
            raw = ring.tile([P, PACK, HALF_H], F32, name="raw", tag="raw", bufs=2 * PASSES, align_bytes=64)
            nc.sync.dma_start(
                out=raw[:], in_=rows[:, HALF_H * half : HALF_H * (half + 1)].rearrange("(p j) c -> p j c", j=PACK)
            )
            return raw

        def load_table(a):
            t = held([P, T], I32, f"table{a}")
            nc.sync.dma_start(out=t[:], in_=tab_words[a].rearrange("p t i -> p (t i)").bitcast(I32))
            return t

        def load_page(g):
            pg = held([P, T2], F32, f"page{g}")
            if g < 2:
                nc.sync.dma_start(out=pg[:], in_=page0.rearrange("(g h m o) c -> g o m h c", g=2, h=2, o=2)[g, 0])
            else:
                nc.sync.dma_start(out=pg[:], in_=page0.rearrange("(p b) c -> b p c", b=PACK)[ODD_BYTE[g]])
            return pg

        def quantise(grouped, name):
            width = grouped.shape[1] // PACK
            codes = held([P, width], U32, name + "_codes")
            scales = held([P, width], U8, name + "_scales")
            nc.vector.quantize_mx(out=codes[:].bitcast(FP8X4), scales=scales[:], in_=grouped)
            return codes, scales

        table_scales = held([P, T], U8, "table_scales")
        nc.vector.memset(table_scales[:].bitcast(I32), 0)
        w4_plane = held([P, N], U8, "w4_plane")
        nc.vector.memset(w4_plane[:].bitcast(I32), 0)

        w1_rows = [w1[K_PASS * a : K_PASS * (a + 1), :] for a in range(PASSES)]
        table = [load_table(0)]
        picks = load_list(offs, "picks")
        for q in range(P // QUAD):
            nc.gpsimd.dma_start(
                out=table_scales[QUAD * q : QUAD * q + 4 * PASSES, :].bitcast(I32),
                in_=tab_scales[:, 4 * q : 4 * q + 4, :].bitcast(I32),
            )
        w1_low = [load_weight(w1_rows[0], 0)]
        table.append(load_table(1))
        w1_low += [load_weight(w1_rows[a], 0) for a in range(1, PASSES)]
        cap_of = [load_even_rows(cap, 0, "cap0")]
        gain_of = [load_even_rows(gain, 0, "gain0")]
        table.append(load_table(2))
        bays = load_list(offs2, "bays")
        wgs_even = held([P, S], F32, "wgs_even")

        def load_wgs_even(half):
            cols = slice(BANK * half, BANK * (half + 1))
            rows = wgs.rearrange("(m o) j -> m o j", o=2)[:, 0:1, cols]
            nc.sync.dma_start(out=wgs_even[:, cols], in_=rows.to_broadcast([HALF_P, 2, BANK]))

        load_wgs_even(0)
        pages = [load_page(0)]
        load_wgs_even(1)
        w1_high = [load_weight(w1_rows[a], 1) for a in range(PASSES)]
        ports = load_list(offs3, "ports")
        stars = load_list(offs4, "stars")
        lean_of = [load_even_rows(lean, 0, "lean0")]
        cap_of.append(load_even_rows(cap, 1, "cap1"))
        gain_of.append(load_even_rows(gain, 1, "gain1"))
        pages.append(load_page(1))
        lean_of.append(load_even_rows(lean, 1, "lean1"))
        cap_of += load_odd_rows(cap, "cap_odd")
        gain_of += load_odd_rows(gain, "gain_odd")
        lean_of += load_odd_rows(lean, "lean_odd")
        wgs_odd = held([P, 2, S], F32, "wgs_odd")
        for q in range(P // QUAD):
            nc.sync.dma_start(
                out=wgs_odd[QUAD * q : QUAD * (q + 1), :, :], in_=wgs.rearrange("(q e o) j -> o q e j", e=2, o=2)[1]
            )
        pages.append(load_page(2))
        pages.append(load_page(3))
        wgs_of = [wgs_even[:], wgs_even[:], wgs_odd[:, 1, :], wgs_odd[:, 0, :]]

        picked = [held([P, S], U32, f"picked{a}") for a in range(PASSES - 1)]
        picked_scales = held([P, S], U8, "picked_scales")
        x_banks = [[psum.tile([P, BANK], F32, name="bank", tag="bank") for half in range(HALVES)] for g in range(PAGES)]

        def first_product(a, g, half, codes, scales, slot):
            rows = slice(P * slot, P * (slot + 1))
            cols = slice(BANK * half, BANK * (half + 1))
            nc.tensor.matmul_mx(
                out=x_banks[g][half][:],
                lhsT=codes[:, rows].bitcast(FP8X4),
                lhsT_scale=scales[:, rows],
                rhs=picked[a][:, cols].bitcast(FP8X4),
                rhs_scale=picked_scales[4 * a : P, cols],
                start=(a == 0),
                stop=(a == PASSES - 1),
            )

        def group_even(dst, raw):
            nc.scalar.copy(
                out=dst.rearrange("p (m i h j) -> p m h j i", i=2, h=2, j=PACK),
                in_=raw[:].rearrange("p j (h m i o) -> p m h j i o", h=2, i=2, o=2)[:, :, :, :, :, 0],
            )

        def group_odd(dst, raw, half):
            nc.scalar.copy(
                out=dst.rearrange("p (e h q j) -> p h q j e", e=2, h=2, j=PACK)[:, half],
                in_=raw[:].rearrange("p j (q e o) -> p q j e o", e=2, o=2)[:, :, :, :, 1],
            )

        grouped_second = held([P, PASSES * K_PASS], BF16, "grouped_second")
        grouped_odd = held([P, PASSES, 2 * K_PASS], BF16, "grouped_odd")
        for a in range(PASSES):
            window = table[a][:].bitcast(U32)
            if a < PASSES - 1:
                nc.vector.tensor_copy(picked[a][:], window.indirect(picks[:]))
            if a == 0:
                nc.vector.tensor_copy(picked_scales[:], table_scales[:].indirect(picks[:]))
            grouped = held([P, K_PASS], BF16, f"grouped_first{a}")
            group_even(grouped[:], w1_low[a])
            codes, scales = quantise(grouped[:], f"w1_first{a}")
            group_odd(grouped_odd[:, a, :], w1_low[a], 0)
            if a == PASSES - 1:
                picked.append(held([P, S], U32, f"picked{a}", tag="table_scales"))
            for half in range(HALVES):
                if a == PASSES - 1:
                    nc.vector.tensor_copy(
                        picked[a][:, BANK * half : BANK * (half + 1)],
                        window.indirect(picks[:, LIST_COLS * half : LIST_COLS * (half + 1)]),
                    )
                first_product(a, 0, half, codes, scales, 0)

        def h_tile():
            return ring.tile([P, S], F32, name="h", tag="h")

        def limit(g, dst, src):
            nc.vector.tensor_scalar(dst, src, cap_of[g], gain_of[g], ALU.min, ALU.mult)

        def evacuate(g):
            h = h_tile()
            for half in range(HALVES):
                nc.scalar.activation(h[:, BANK * half : BANK * (half + 1)], x_banks[g][half][:], IDENTITY)
            return h

        h_first = h_tile()
        limit(0, h_first[:, 0:BANK], x_banks[0][0][:])
        h_second = h_tile()
        nc.scalar.activation(h_second[:, 0:BANK], x_banks[0][1][:], IDENTITY)
        nc.vector.tensor_tensor(pages[0][:].indirect(bays[:, 0:LIST_COLS]), h_first[:, 0:BANK], wgs_of[0][:, 0:BANK], ALU.mult)
        limit(0, h_second[:, 0:BANK], h_second[:, 0:BANK])
        nc.vector.tensor_tensor(
            pages[0][:].indirect(bays[:, LIST_COLS : 2 * LIST_COLS]), h_second[:, 0:BANK], wgs_of[0][:, BANK:S], ALU.mult
        )

        lean_less_one = held([P, PAGES], F32, "lean_less_one")
        for g in range(PAGES):
            nc.scalar.activation(lean_less_one[:, g : g + 1], lean_of[g], COPY, bias=-1.0)

        for a in range(PASSES):
            group_even(grouped_second[:, K_PASS * a : K_PASS * (a + 1)], w1_high[a])
        codes, scales = quantise(grouped_second[:], "w1_second")
        for half in range(HALVES):
            for a in range(PASSES):
                first_product(a, 1, half, codes, scales, a)
        for a in range(PASSES):
            group_odd(grouped_odd[:, a, :], w1_high[a], 1)
        odd_front = quantise(grouped_odd[:, 0:2, :].rearrange("p a c -> p (a c)"), "w1_odd_front")
        odd_back = quantise(grouped_odd[:, 2, :], "w1_odd_back")
        for g, slot in ((2, 1), (3, 0)):
            for half in range(HALVES):
                for a in range(PASSES):
                    codes, scales = odd_front if a < 2 else odd_back
                    first_product(a, g, half, codes, scales, 2 * (a % 2) + slot)
        h = {1: evacuate(1)}

        w5_raw = [load_weight(w5, half) for half in range(2)]
        w4_sb = held([P, 2 * N], U8, "w4")
        nc.sync.dma_start(out=w4_sb[:].bitcast(I32), in_=w4_words[0].bitcast(I32))
        for q in range(P // QUAD):
            nc.sync.dma_start(
                out=w4_plane[QUAD * q : QUAD * q + 4, :].bitcast(I32),
                in_=w4_scales[0, 4 * q : 4 * q + 4, :].bitcast(I32),
            )
        bias_sb = held([P, N // P], F32, "bias")
        with nc.allow_non_contiguous_dma(reason="one bias value to a partition"):
            nc.sync.dma_start(out=bias_sb[:], in_=bias.rearrange("(j p) -> p j", p=P))

        w5_grouped = held([P, PACK * N], BF16, "w5_grouped")
        deck = [held([P, BANK, PACK], BF16, f"deck{c}") for c in range(CHUNKS)]
        moved = [held([P, 2, T2 // 2], F32, f"moved{half}") for half in range(2)]

        def round_rows(copy, g, c):
            copy(out=deck[c][:, :, ODD_BYTE[g]], in_=pages[g][:, BANK * c : BANK * (c + 1)])

        w5_mx = []

        def quantise_w5():
            j = len(w5_mx)
            w5_mx.append(quantise(w5_grouped[:, K_PASS * j : K_PASS * (j + 1)], f"w5_{j}"))

        def quantise_deck(c):
            return quantise(deck[c][:].rearrange("p c t -> p (c t)"), f"deck{c}")

        for g in range(PAGES):
            if g == 0:
                port = held([P, PAIRS], F32, "port_first", tag="grouped_second")[:]
                star, rise = [ring.tile([P, PAIRS], F32, name=n, tag=n)[:] for n in ("star", "rise")]
            elif g == PAGES - 1:
                port = held([P, PAIRS], F32, "port_last", tag="moved0")[:]
                last = held([P, 2, PAIRS], F32, "pair_last", tag="moved1")
                star, rise = last[:, 0, :], last[:, 1, :]
            else:
                port, star, rise = [ring.tile([P, PAIRS], F32, name=n, tag=n)[:] for n in ("port", "star", "rise")]
            nc.vector.tensor_copy(port, pages[g][:].indirect(ports[:]))
            nc.vector.tensor_copy(star, pages[g][:].indirect(stars[:]))
            if g + 1 < PAGES:
                limit(g + 1, h[g + 1][:], h[g + 1][:])
            if g + 2 < PAGES:
                h[g + 2] = evacuate(g + 2)
            if g == 1:
                for half in range(2):
                    nc.scalar.copy(
                        out=w5_grouped[:, 2 * N * half : 2 * N * (half + 1)].rearrange("p (c i j) -> p c j i", i=4, j=PACK),
                        in_=w5_raw[half][:].rearrange("p j (c i) -> p c j i", i=4),
                    )
            if g == PAGES - 1:
                quantise_w5()
            nc.vector.scalar_tensor_tensor(rise, port, lean_less_one[:, g : g + 1], star, ALU.mult, ALU.max)
            nc.vector.tensor_tensor(pages[g][:].indirect(ports[:]), port, star, ALU.add)
            if g + 1 < PAGES:
                nc.vector.tensor_tensor(pages[g + 1][:].indirect(bays[:]), h[g + 1][:], wgs_of[g + 1], ALU.mult)
            else:
                quantise_w5()
            nc.vector.tensor_tensor(pages[g][:].indirect(stars[:]), port, rise, ALU.add)
            if g < 2:
                for half in range(2):
                    cols = slice(T2 // 2 * half, T2 // 2 * (half + 1))
                    for low in range(2):
                        first_row = QUAD * (2 * g + low)
                        nc.scalar.dma_start(out=moved[half][first_row : first_row + QUAD, :, :], in_=pages[g][low:P:2, cols])
            if g == 1:
                for c in range(CHUNKS):
                    nc.scalar.copy(
                        out=deck[c][:].rearrange("p c (u o) -> p c u o", o=2)[:, :, :, 0],
                        in_=moved[c // 2][:, :, BANK * (c % 2) : BANK * (c % 2 + 1)].rearrange("p u c -> p c u"),
                    )
            if g == 2:
                for c in range(CHUNKS):
                    round_rows(nc.scalar.copy, g, c)

        quantise_w5()
        round_rows(nc.vector.tensor_copy, PAGES - 1, 0)
        for c in range(1, CHUNKS - 1):
            round_rows(nc.scalar.copy, PAGES - 1, c)
        quantise_w5()
        deck_mx = [quantise_deck(0)]
        round_rows(nc.vector.tensor_copy, PAGES - 1, CHUNKS - 1)
        deck_mx += [quantise_deck(c) for c in range(1, CHUNKS)]
        for c in range(CHUNKS):
            codes, scales = deck_mx[c]
            for j in range(N // P):
                rows = slice(P * j, P * (j + 1))
                y4 = psum.tile([P, BANK], F32, name="bank", tag="bank")
                nc.tensor.matmul_mx(
                    out=y4[:],
                    lhsT=w4_sb[:, 2 * P * j : 2 * P * (j + 1)].bitcast(FP4X4),
                    lhsT_scale=w4_plane[:, rows],
                    rhs=codes[:].bitcast(FP8X4),
                    rhs_scale=scales[:],
                    start=True,
                    stop=True,
                )
                y5 = psum.tile([P, BANK], F32, name="bank", tag="bank")
                nc.tensor.matmul_mx(
                    out=y5[:],
                    lhsT=w5_mx[j][0][:].bitcast(FP8X4),
                    lhsT_scale=w5_mx[j][1][:],
                    rhs=codes[:].bitcast(FP8X4),
                    rhs_scale=scales[:],
                    start=True,
                    stop=True,
                )
                first = ring.tile([P, BANK], F32, name="first", tag="first", bufs=4)
                nc.scalar.activation(first[:], y4[:], IDENTITY, bias=bias_sb[:, j : j + 1])
                result = ring.tile([P, BANK], F32, name="result", tag="raw", bufs=2 * PASSES, align_bytes=64)
                nc.vector.scalar_tensor_tensor(result[:], y5[:], bias_sb[:, j : j + 1], first[:], ALU.add, ALU.max)
                nc.sync.dma_start(out=out[rows, BANK * c : BANK * (c + 1)], in_=result[:])
